import numpy as np
import ml_dtypes


def mxq(x, axis, fmt="e4m3"):
    dtype, down = {"e4m3": (ml_dtypes.float8_e4m3fn, 7), "e5m2": (ml_dtypes.float8_e5m2, 14)}[fmt]
    v = np.moveaxis(np.asarray(x, np.float32).astype(ml_dtypes.bfloat16).astype(np.float64), axis, -1)
    blocks = v.reshape(v.shape[:-1] + (-1, 32))
    amax = np.abs(blocks).max(-1, keepdims=True)
    byte = np.maximum(np.where(amax > 0, np.frexp(amax)[1] - 1 + 127, 0) - down, 1)
    scale = np.exp2(byte - 127.0)
    codes = (blocks / scale).astype(np.float32).astype(dtype).astype(np.float64)
    return np.moveaxis((codes * scale).reshape(v.shape), -1, axis)


WIDE = False


def mx_kscale(k):
    if not WIDE:
        return np.ones(k)
    levels = np.array([10, -10, 5, -5, 0])
    if k % 512:
        return np.exp2(np.random.permutation(np.resize(levels, k // 32))).repeat(32)
    a = np.empty((k // 512, 16))
    for p in range(k // 512):
        a[p, :8] = np.random.permutation(np.resize(levels, 8))
        for g in range(8):
            far = levels[np.abs(levels - a[p, g]) >= 10]
            a[p, g + 8] = far[np.random.randint(len(far))]
    return np.exp2(a.ravel()).repeat(32)


def f64(x):
    return np.asarray(x).astype(np.float64)


def striped(idx):
    return np.tile(np.asarray(idx).reshape(-1, 16).T, (8, 1)).astype(np.uint16)


def unstriped(offs):
    return offs[:16].T.reshape(-1).astype(np.int64)


E2M1 = np.array([0.0, 0.5, 1.0, 1.5, 2.0, 3.0, 4.0, 6.0, -0.0, -0.5, -1.0, -1.5, -2.0, -3.0, -4.0, -6.0])


def pack_weight(w, fmt):
    k, n = w.shape
    w = f64(np.asarray(w, np.float32).astype(ml_dtypes.bfloat16)).reshape(k // 32, 32, n)
    amax = np.abs(w).max(1)
    if fmt == "e4m3":
        byte = np.frexp(amax)[1] - 1 + 127 - 7
    else:
        mant, ex = np.frexp(amax / 6.0)
        byte = np.where(mant > 0.5, ex, ex - 1) + 127
    byte = np.clip(np.where(amax > 0, byte, 1), 1, 254)
    scaled = (w * np.exp2(127.0 - byte)[:, None, :]).reshape(k, n).astype(np.float32)
    by_word = np.ascontiguousarray(scaled.reshape(k // 512, 128, 4, n).transpose(0, 1, 3, 2))
    if fmt == "e4m3":
        words = by_word.astype(ml_dtypes.float8_e4m3fn).view(np.uint8)
    else:
        c = by_word.astype(ml_dtypes.float4_e2m1fn).view(np.uint8) & 0xF
        words = (c[..., 0::2] | (c[..., 1::2] << 4)).reshape(k // 512, 128, 2 * n)
    return np.ascontiguousarray(words), np.ascontiguousarray(byte.astype(np.uint8).reshape(k // 512, 16, n))


def unpack_weight(words, scales, fmt):
    g, _, n = scales.shape
    words = np.ascontiguousarray(words).reshape(g, 128, n, -1)
    if fmt == "e4m3":
        vals = words.view(ml_dtypes.float8_e4m3fn).astype(np.float64)
    else:
        nib = np.empty((g, 128, n, 4), np.uint8)
        nib[..., 0::2] = words & 0xF
        nib[..., 1::2] = words >> 4
        vals = E2M1[nib]
    vals = vals * np.repeat(np.exp2(scales.astype(np.float64) - 127.0), 8, axis=1)[..., None]
    return vals.transpose(0, 1, 3, 2).reshape(g * 512, n)


B, N, T, D, DV, NQ = 1, 512, 2048, 1024, 0, 128
PAGE = 32
SEG = 32


def setup_inputs():
    n = np.random.standard_normal
    pages = np.random.permutation(T // PAGE)[:B * N // PAGE]
    idx = (pages[:, None] * PAGE + np.arange(PAGE)[None, :]).reshape(-1)
    s = mx_kscale(D)[:, None]
    kp = pack_weight(n((D, T)) / s, "e2m1")
    return {
        "qT": (n((B, D, NQ)) * s * (1.00 / np.sqrt(D))).astype(np.float32),
        "k_words": np.ascontiguousarray(kp[0].reshape(1, 2, 128, T, 2).transpose(0, 2, 3, 1, 4)).reshape(1, 128, T, 4),
        "k_scales": kp[1],
        "offs": striped(idx),
    }


def reference(qT, k_words, k_scales, offs):
    idx = unstriped(offs)
    pool = unpack_weight(k_words.reshape(1, 128, T, 2, 2).transpose(0, 3, 1, 2, 4).reshape(2, 128, 2 * T), k_scales, "e2m1")
    pick = lambda x: x[:, idx].reshape(x.shape[0], B, N).transpose(1, 0, 2)
    a = mxq(f64(qT), 1, "e4m3").transpose(0, 2, 1) @ pick(pool)
    return a.reshape(B, NQ, N // SEG, SEG).max(-1)

@@ -1,0 +1,99 @@
+from contextlib import ExitStack
+
+import concourse.mybir as mybir
+
+F32 = mybir.dt.float32
+BF16 = mybir.dt.bfloat16
+I32 = mybir.dt.int32
+U32 = mybir.dt.uint32
+U16 = mybir.dt.uint16
+U8 = mybir.dt.uint8
+FP8X4 = mybir.dt.float8_e4m3fn_x4
+FP4X4 = mybir.dt.float4_e2m1fn_x4
+
+P = 128
+N, T, D, NQ, SEG = 512, 2048, 1024, 128, 32
+PASSES = 2
+HALF = N // 2
+CH = 128
+FLOPS = 2 * NQ * N * D
+
+
+def tile_attend_maxsim_kernel(tc, qT, k_words, k_scales, offs, out):
+    nc = tc.nc
+    with ExitStack() as ctx:
+        sb = ctx.enter_context(tc.tile_pool(name="sb", bufs=1))
+        ps = ctx.enter_context(tc.psum_pool(name="ps", bufs=1))
+
+        offsets = sb.tile([P, N // 16], U16, name="offsets")
+        nc.sync.dma_start(offsets[:], offs)
+
+        word_pool = sb.tile([P, T], I32, name="word_pool", align_bytes=64)
+        nc.scalar.dma_start(word_pool[:], k_words[0].rearrange("p t b -> p (t b)").bitcast(I32))
+        q_raw = []
+        for o in range(PASSES):
+            raw = sb.tile([P, 4, NQ], F32, name="q_raw%d" % o, align_bytes=64)
+            nc.scalar.dma_start(raw[:], qT[0, 512 * o : 512 * (o + 1), :].rearrange("(p j) w -> p j w", j=4))
+            q_raw.append(raw)
+
+        scale_pool = sb.tile([P, T], U8, name="scale_pool", align_bytes=64)
+        nc.vector.memset(scale_pool[:].bitcast(I32), 0)
+        nc.sync.dma_start(scale_pool[0:P:4, :].bitcast(I32), k_scales.rearrange("o f t -> f o t").bitcast(I32))
+        k_planes = sb.tile([P, PASSES * N], U8, name="k_planes", align_bytes=64)
+        nc.vector.memset(k_planes[:].bitcast(I32), 0)
+
+        scale_got = sb.tile([P, N], U8, name="scale_got", align_bytes=64)
+        nc.vector.tensor_copy(scale_got[:], scale_pool[:].indirect(offsets[:]))
+        for quad in range(4):
+            nc.sync.dma_start(
+                k_planes[32 * quad : 32 * quad + 4, :].bitcast(I32),
+                scale_got[32 * quad : 32 * quad + 32 : 4, :].bitcast(I32),
+            )
+
+        word_got = sb.tile([P, N], U32, name="word_got", align_bytes=64)
+        for h in range(2):
+            nc.vector.tensor_copy(
+                word_got[:, h * HALF : (h + 1) * HALF],
+                word_pool[:].bitcast(U32).indirect(offsets[:, h * HALF // 16 : (h + 1) * HALF // 16]),
+            )
+        k_codes = sb.tile([P, PASSES * 2 * N], U8, name="k_codes", align_bytes=64)
+        for h in range(2):
+            nc.vector.tensor_copy(
+                k_codes[:].bitcast(U16).rearrange("p (o n) -> p o n", o=PASSES)[:, :, h * HALF : (h + 1) * HALF],
+                word_got[:, h * HALF : (h + 1) * HALF].bitcast(U16).rearrange("p (n o) -> p o n", o=PASSES),
+            )
+
+        q_codes = sb.tile([P, PASSES * NQ], U32, name="q_codes", align_bytes=64)
+        q_planes = sb.tile([P, PASSES * NQ], U8, name="q_planes", align_bytes=64)
+        for o in range(PASSES):
+            grouped = sb.tile([P, NQ, 4], BF16, name="q_bf%d" % o, align_bytes=64)
+            nc.scalar.copy(grouped[:], q_raw[o][:].rearrange("p j w -> p w j"))
+            nc.vector.quantize_mx(
+                out=q_codes[:, o * NQ : (o + 1) * NQ].bitcast(FP8X4),
+                scales=q_planes[:, o * NQ : (o + 1) * NQ],
+                in_=grouped[:].rearrange("p w j -> p (w j)"),
+            )
+
+        banks = [ps.tile([P, CH], F32, name="bank%d" % g) for g in range(N // CH)]
+        best = sb.tile([P, N // SEG], F32, name="best", align_bytes=64)
+        for o in range(PASSES):
+            for g in range(N // CH):
+                c0 = o * N + g * CH
+                nc.tensor.matmul_mx(
+                    out=banks[g][:],
+                    lhsT=q_codes[:, o * NQ : (o + 1) * NQ].bitcast(FP8X4),
+                    lhsT_scale=q_planes[:, o * NQ : (o + 1) * NQ],
+                    rhs=k_codes[:, 2 * c0 : 2 * (c0 + CH)].bitcast(FP4X4),
+                    rhs_scale=k_planes[:, c0 : c0 + CH],
+                    start=(o == 0),
+                    stop=(o == PASSES - 1),
+                )
+        per = CH // SEG
+        for g in range(N // CH):
+            nc.vector.tensor_reduce(
+                out=best[:, g * per : (g + 1) * per],
+                in_=banks[g][:].rearrange("p (j s) -> p j s", s=SEG),
+                axis=mybir.AxisListType.X,
+                op=mybir.AluOpType.max,
+            )
+        nc.sync.dma_start(out[0], best[:])

@@ -28,17 +28,18 @@ def tile_attend_maxsim_kernel(tc, qT, k_words, k_scales, offs, out):
         offsets = sb.tile([P, N // 16], U16, name="offsets")
         nc.sync.dma_start(offsets[:], offs)
 
+        scale_pool = sb.tile([P, T], U8, name="scale_pool", align_bytes=64)
+        nc.scalar.dma_start(scale_pool[96:P, :].bitcast(I32), k_scales.rearrange("o f t -> f o t").bitcast(I32))
         word_pool = sb.tile([P, T], I32, name="word_pool", align_bytes=64)
-        nc.scalar.dma_start(word_pool[:], k_words[0].rearrange("p t b -> p (t b)").bitcast(I32))
         q_raw = []
         for o in range(PASSES):
             raw = sb.tile([P, 4, NQ], F32, name="q_raw%d" % o, align_bytes=64)
             nc.scalar.dma_start(raw[:], qT[0, 512 * o : 512 * (o + 1), :].rearrange("(p j) w -> p j w", j=4))
             q_raw.append(raw)
+            if o == 0:
+                nc.scalar.dma_start(word_pool[:], k_words[0].rearrange("p t b -> p (t b)").bitcast(I32))
 
-        scale_pool = sb.tile([P, T], U8, name="scale_pool", align_bytes=64)
-        nc.vector.memset(scale_pool[:].bitcast(I32), 0)
-        nc.sync.dma_start(scale_pool[0:P:4, :].bitcast(I32), k_scales.rearrange("o f t -> f o t").bitcast(I32))
+        nc.vector.memset(scale_pool[0:96, :].bitcast(I32), 0)
         k_planes = sb.tile([P, PASSES * N], U8, name="k_planes", align_bytes=64)
         nc.vector.memset(k_planes[:].bitcast(I32), 0)
 
@@ -47,7 +48,7 @@ def tile_attend_maxsim_kernel(tc, qT, k_words, k_scales, offs, out):
         for quad in range(4):
             nc.sync.dma_start(
                 k_planes[32 * quad : 32 * quad + 4, :].bitcast(I32),
-                scale_got[32 * quad : 32 * quad + 32 : 4, :].bitcast(I32),
+                scale_got[96 + 8 * quad : 104 + 8 * quad, :].bitcast(I32),
             )
 
         word_got = sb.tile([P, N], U32, name="word_got", align_bytes=64)
@@ -57,17 +58,21 @@ def tile_attend_maxsim_kernel(tc, qT, k_words, k_scales, offs, out):
                 word_pool[:].bitcast(U32).indirect(offsets[:, h * HALF // 16 : (h + 1) * HALF // 16]),
             )
         k_codes = sb.tile([P, PASSES * 2 * N], U8, name="k_codes", align_bytes=64)
-        for h in range(2):
-            nc.vector.tensor_copy(
-                k_codes[:].bitcast(U16).rearrange("p (o n) -> p o n", o=PASSES)[:, :, h * HALF : (h + 1) * HALF],
-                word_got[:, h * HALF : (h + 1) * HALF].bitcast(U16).rearrange("p (n o) -> p o n", o=PASSES),
-            )
+        for o in range(PASSES):
+            for h in range(2):
+                nc.vector.tensor_copy(
+                    k_codes[:].bitcast(U16)[:, o * N + h * HALF : o * N + (h + 1) * HALF],
+                    word_got[:, h * HALF : (h + 1) * HALF].bitcast(U16).rearrange("p (n o) -> p o n", o=PASSES)[:, o, :],
+                )
 
         q_codes = sb.tile([P, PASSES * NQ], U32, name="q_codes", align_bytes=64)
         q_planes = sb.tile([P, PASSES * NQ], U8, name="q_planes", align_bytes=64)
         for o in range(PASSES):
             grouped = sb.tile([P, NQ, 4], BF16, name="q_bf%d" % o, align_bytes=64)
-            nc.scalar.copy(grouped[:], q_raw[o][:].rearrange("p j w -> p w j"))
+            nc.scalar.copy(
+                grouped[:].rearrange("p (c i) j -> p c j i", i=4),
+                q_raw[o][:].rearrange("p j (c i) -> p c j i", i=4),
+            )
             nc.vector.quantize_mx(
                 out=q_codes[:, o * NQ : (o + 1) * NQ].bitcast(FP8X4),
                 scales=q_planes[:, o * NQ : (o + 1) * NQ],

@@ -31,13 +31,17 @@ def tile_attend_maxsim_kernel(tc, qT, k_words, k_scales, offs, out):
         scale_pool = sb.tile([P, T], U8, name="scale_pool", align_bytes=64)
         nc.scalar.dma_start(scale_pool[96:P, :].bitcast(I32), k_scales.rearrange("o f t -> f o t").bitcast(I32))
         word_pool = sb.tile([P, T], I32, name="word_pool", align_bytes=64)
+        nc.scalar.dma_start(word_pool[:], k_words[0].rearrange("p t b -> p (t b)").bitcast(I32))
         q_raw = []
         for o in range(PASSES):
-            raw = sb.tile([P, 4, NQ], F32, name="q_raw%d" % o, align_bytes=64)
+            raw = sb.tile([P, 4, NQ], F32, name="q_raw%d" % o, tag="stage%d" % o, align_bytes=64)
             nc.scalar.dma_start(raw[:], qT[0, 512 * o : 512 * (o + 1), :].rearrange("(p j) w -> p j w", j=4))
             q_raw.append(raw)
-            if o == 0:
-                nc.scalar.dma_start(word_pool[:], k_words[0].rearrange("p t b -> p (t b)").bitcast(I32))
+
+        warm_in = sb.tile([P, 1], F32, name="warm_in")
+        warm_out = sb.tile([P, 1], F32, name="warm_out")
+        nc.gpsimd.memset(warm_in[:], 0.0)
+        nc.scalar.copy(warm_out[:], warm_in[:])
 
         nc.vector.memset(scale_pool[0:96, :].bitcast(I32), 0)
         k_planes = sb.tile([P, PASSES * N], U8, name="k_planes", align_bytes=64)
@@ -46,7 +50,7 @@ def tile_attend_maxsim_kernel(tc, qT, k_words, k_scales, offs, out):
         scale_got = sb.tile([P, N], U8, name="scale_got", align_bytes=64)
         nc.vector.tensor_copy(scale_got[:], scale_pool[:].indirect(offsets[:]))
         for quad in range(4):
-            nc.sync.dma_start(
+            (nc.sync, nc.scalar)[quad % 2].dma_start(
                 k_planes[32 * quad : 32 * quad + 4, :].bitcast(I32),
                 scale_got[96 + 8 * quad : 104 + 8 * quad, :].bitcast(I32),
             )
@@ -57,17 +61,15 @@ def tile_attend_maxsim_kernel(tc, qT, k_words, k_scales, offs, out):
                 word_got[:, h * HALF : (h + 1) * HALF],
                 word_pool[:].bitcast(U32).indirect(offsets[:, h * HALF // 16 : (h + 1) * HALF // 16]),
             )
-        k_codes = sb.tile([P, PASSES * 2 * N], U8, name="k_codes", align_bytes=64)
-        for o in range(PASSES):
-            for h in range(2):
-                nc.vector.tensor_copy(
-                    k_codes[:].bitcast(U16)[:, o * N + h * HALF : o * N + (h + 1) * HALF],
-                    word_got[:, h * HALF : (h + 1) * HALF].bitcast(U16).rearrange("p (n o) -> p o n", o=PASSES)[:, o, :],
-                )
-
         q_codes = sb.tile([P, PASSES * NQ], U32, name="q_codes", align_bytes=64)
         q_planes = sb.tile([P, PASSES * NQ], U8, name="q_planes", align_bytes=64)
-        for o in range(PASSES):
+
+        word_halves = word_got[:].bitcast(U16).rearrange("p (n o) -> p o n", o=PASSES)
+
+        def part_words(codes, o, lo, hi):
+            nc.vector.tensor_copy(codes.bitcast(U16), word_halves[:, o, lo:hi])
+
+        def quantise_queries(o):
             grouped = sb.tile([P, NQ, 4], BF16, name="q_bf%d" % o, align_bytes=64)
             nc.scalar.copy(
                 grouped[:].rearrange("p (c i) j -> p c j i", i=4),
@@ -79,6 +81,19 @@ def tile_attend_maxsim_kernel(tc, qT, k_words, k_scales, offs, out):
                 in_=grouped[:].rearrange("p w j -> p (w j)"),
             )
 
+        k_first = sb.tile([P, 2 * HALF], U8, name="k_first", align_bytes=64)
+        part_words(k_first[:], 0, 0, HALF)
+        quantise_queries(0)
+        k_rest = sb.tile([P, 2 * HALF + 2 * N], U8, name="k_rest", tag="stage0", align_bytes=64)
+        part_words(k_rest[:, : 2 * HALF], 0, HALF, N)
+        part_words(k_rest[:, 2 * HALF :], 1, 0, N)
+        quantise_queries(1)
+
+        def k_codes(c0):
+            if c0 < HALF:
+                return k_first[:, 2 * c0 : 2 * (c0 + CH)]
+            return k_rest[:, 2 * (c0 - HALF) : 2 * (c0 - HALF + CH)]
+
         banks = [ps.tile([P, CH], F32, name="bank%d" % g) for g in range(N // CH)]
         best = sb.tile([P, N // SEG], F32, name="best", align_bytes=64)
         for o in range(PASSES):
@@ -88,7 +103,7 @@ def tile_attend_maxsim_kernel(tc, qT, k_words, k_scales, offs, out):
                     out=banks[g][:],
                     lhsT=q_codes[:, o * NQ : (o + 1) * NQ].bitcast(FP8X4),
                     lhsT_scale=q_planes[:, o * NQ : (o + 1) * NQ],
-                    rhs=k_codes[:, 2 * c0 : 2 * (c0 + CH)].bitcast(FP4X4),
+                    rhs=k_codes(c0).bitcast(FP4X4),
                     rhs_scale=k_planes[:, c0 : c0 + CH],
                     start=(o == 0),
                     stop=(o == PASSES - 1),

@@ -84,14 +84,18 @@ def tile_attend_maxsim_kernel(tc, qT, k_words, k_scales, offs, out):
         k_first = sb.tile([P, 2 * HALF], U8, name="k_first", align_bytes=64)
         part_words(k_first[:], 0, 0, HALF)
         quantise_queries(0)
-        k_rest = sb.tile([P, 2 * HALF + 2 * N], U8, name="k_rest", tag="stage0", align_bytes=64)
+        k_rest = sb.tile([P, 2 * N], U8, name="k_rest", tag="stage0", align_bytes=64)
         part_words(k_rest[:, : 2 * HALF], 0, HALF, N)
-        part_words(k_rest[:, 2 * HALF :], 1, 0, N)
+        part_words(k_rest[:, 2 * HALF :], 1, 0, HALF)
         quantise_queries(1)
+        k_last = sb.tile([P, 2 * HALF], U8, name="k_last", tag="stage1", align_bytes=64)
+        part_words(k_last[:], 1, HALF, N)
 
         def k_codes(c0):
             if c0 < HALF:
                 return k_first[:, 2 * c0 : 2 * (c0 + CH)]
+            if c0 >= N + HALF:
+                return k_last[:, 2 * (c0 - N - HALF) : 2 * (c0 - N - HALF + CH)]
             return k_rest[:, 2 * (c0 - HALF) : 2 * (c0 - HALF + CH)]
 
         banks = [ps.tile([P, CH], F32, name="bank%d" % g) for g in range(N // CH)]

@@ -29,13 +29,13 @@ def tile_attend_maxsim_kernel(tc, qT, k_words, k_scales, offs, out):
         nc.sync.dma_start(offsets[:], offs)
 
         scale_pool = sb.tile([P, T], U8, name="scale_pool", align_bytes=64)
-        nc.scalar.dma_start(scale_pool[96:P, :].bitcast(I32), k_scales.rearrange("o f t -> f o t").bitcast(I32))
+        nc.sync.dma_start(scale_pool[96:P, :].bitcast(I32), k_scales.rearrange("o f t -> f o t").bitcast(I32))
         word_pool = sb.tile([P, T], I32, name="word_pool", align_bytes=64)
-        nc.scalar.dma_start(word_pool[:], k_words[0].rearrange("p t b -> p (t b)").bitcast(I32))
+        nc.sync.dma_start(word_pool[:], k_words[0].rearrange("p t b -> p (t b)").bitcast(I32))
         q_raw = []
         for o in range(PASSES):
             raw = sb.tile([P, 4, NQ], F32, name="q_raw%d" % o, tag="stage%d" % o, align_bytes=64)
-            nc.scalar.dma_start(raw[:], qT[0, 512 * o : 512 * (o + 1), :].rearrange("(p j) w -> p j w", j=4))
+            nc.sync.dma_start(raw[:], qT[0, 512 * o : 512 * (o + 1), :].rearrange("(p j) w -> p j w", j=4))
             q_raw.append(raw)
 
         warm_in = sb.tile([P, 1], F32, name="warm_in")
@@ -50,7 +50,7 @@ def tile_attend_maxsim_kernel(tc, qT, k_words, k_scales, offs, out):
         scale_got = sb.tile([P, N], U8, name="scale_got", align_bytes=64)
         nc.vector.tensor_copy(scale_got[:], scale_pool[:].indirect(offsets[:]))
         for quad in range(4):
-            (nc.sync, nc.scalar)[quad % 2].dma_start(
+            nc.sync.dma_start(
                 k_planes[32 * quad : 32 * quad + 4, :].bitcast(I32),
                 scale_got[96 + 8 * quad : 104 + 8 * quad, :].bitcast(I32),
             )

@@ -38,11 +38,6 @@ def tile_attend_maxsim_kernel(tc, qT, k_words, k_scales, offs, out):
             nc.sync.dma_start(raw[:], qT[0, 512 * o : 512 * (o + 1), :].rearrange("(p j) w -> p j w", j=4))
             q_raw.append(raw)
 
-        warm_in = sb.tile([P, 1], F32, name="warm_in")
-        warm_out = sb.tile([P, 1], F32, name="warm_out")
-        nc.gpsimd.memset(warm_in[:], 0.0)
-        nc.scalar.copy(warm_out[:], warm_in[:])
-
         nc.vector.memset(scale_pool[0:96, :].bitcast(I32), 0)
         k_planes = sb.tile([P, PASSES * N], U8, name="k_planes", align_bytes=64)
         nc.vector.memset(k_planes[:].bitcast(I32), 0)

@@ -16,6 +16,7 @@ N, T, D, NQ, SEG = 512, 2048, 1024, 128, 32
 PASSES = 2
 HALF = N // 2
 CH = 128
+SCALAR_SHARE = 96
 FLOPS = 2 * NQ * N * D
 
 
@@ -66,10 +67,16 @@ def tile_attend_maxsim_kernel(tc, qT, k_words, k_scales, offs, out):
 
         def quantise_queries(o):
             grouped = sb.tile([P, NQ, 4], BF16, name="q_bf%d" % o, align_bytes=64)
+            own = SCALAR_SHARE if o == 1 else NQ
             nc.scalar.copy(
-                grouped[:].rearrange("p (c i) j -> p c j i", i=4),
-                q_raw[o][:].rearrange("p j (c i) -> p c j i", i=4),
+                grouped[:, :own, :].rearrange("p (c i) j -> p c j i", i=4),
+                q_raw[o][:, :, :own].rearrange("p j (c i) -> p c j i", i=4),
             )
+            if own < NQ:
+                nc.vector.tensor_copy(
+                    grouped[:, own:, :].rearrange("p (c i) j -> p c j i", i=4),
+                    q_raw[o][:, :, own:].rearrange("p j (c i) -> p c j i", i=4),
+                )
             nc.vector.quantize_mx(
                 out=q_codes[:, o * NQ : (o + 1) * NQ].bitcast(FP8X4),
                 scales=q_planes[:, o * NQ : (o + 1) * NQ],

@@ -45,7 +45,7 @@ def tile_attend_maxsim_kernel(tc, qT, k_words, k_scales, offs, out):
 
         scale_got = sb.tile([P, N], U8, name="scale_got", align_bytes=64)
         nc.vector.tensor_copy(scale_got[:], scale_pool[:].indirect(offsets[:]))
-        for quad in range(4):
+        for quad in (0, 2, 1, 3):
             nc.sync.dma_start(
                 k_planes[32 * quad : 32 * quad + 4, :].bitcast(I32),
                 scale_got[96 + 8 * quad : 104 + 8 * quad, :].bitcast(I32),

@@ -45,11 +45,16 @@ def tile_attend_maxsim_kernel(tc, qT, k_words, k_scales, offs, out):
 
         scale_got = sb.tile([P, N], U8, name="scale_got", align_bytes=64)
         nc.vector.tensor_copy(scale_got[:], scale_pool[:].indirect(offsets[:]))
-        for quad in (0, 2, 1, 3):
-            nc.sync.dma_start(
-                k_planes[32 * quad : 32 * quad + 4, :].bitcast(I32),
-                scale_got[96 + 8 * quad : 104 + 8 * quad, :].bitcast(I32),
-            )
+        planes = k_planes[:].bitcast(I32)
+        staged = scale_got[:].bitcast(I32)
+        for quad in (0, 2):
+            nc.sync.dma_start(planes[32 * quad : 32 * quad + 4, :], staged[96 + 8 * quad : 104 + 8 * quad, :])
+        for o in range(PASSES):
+            for quad in (1, 3):
+                nc.sync.dma_start(
+                    planes[32 * quad : 32 * quad + 4, o * N // 4 : (o + 1) * N // 4],
+                    staged[96 + 8 * quad + o : 104 + 8 * quad : 2, :],
+                )
 
         word_got = sb.tile([P, N], U32, name="word_got", align_bytes=64)
         for h in range(2):

@@ -47,14 +47,21 @@ def tile_attend_maxsim_kernel(tc, qT, k_words, k_scales, offs, out):
         nc.vector.tensor_copy(scale_got[:], scale_pool[:].indirect(offsets[:]))
         planes = k_planes[:].bitcast(I32)
         staged = scale_got[:].bitcast(I32)
+
+        def move_rows(quad, o, lo, hi):
+            nc.sync.dma_start(
+                planes[32 * quad : 32 * quad + 4, (o * N + lo) // 4 : (o * N + hi) // 4],
+                staged[96 + 8 * quad + o : 104 + 8 * quad : 2, lo // 4 : hi // 4],
+            )
+
         for quad in (0, 2):
             nc.sync.dma_start(planes[32 * quad : 32 * quad + 4, :], staged[96 + 8 * quad : 104 + 8 * quad, :])
-        for o in range(PASSES):
-            for quad in (1, 3):
-                nc.sync.dma_start(
-                    planes[32 * quad : 32 * quad + 4, o * N // 4 : (o + 1) * N // 4],
-                    staged[96 + 8 * quad + o : 104 + 8 * quad : 2, :],
-                )
+        move_rows(1, 0, 0, N)
+        move_rows(3, 0, 0, N)
+        move_rows(1, 1, 0, N)
+        cuts = [0, 2 * CH, N]
+        for lo, hi in zip(cuts, cuts[1:]):
+            move_rows(3, 1, lo, hi)
 
         word_got = sb.tile([P, N], U32, name="word_got", align_bytes=64)
         for h in range(2):

@@ -30,7 +30,7 @@ def tile_attend_maxsim_kernel(tc, qT, k_words, k_scales, offs, out):
         nc.sync.dma_start(offsets[:], offs)
 
         scale_pool = sb.tile([P, T], U8, name="scale_pool", align_bytes=64)
-        nc.sync.dma_start(scale_pool[96:P, :].bitcast(I32), k_scales.rearrange("o f t -> f o t").bitcast(I32))
+        nc.sync.dma_start(scale_pool[0:32, :].bitcast(I32), k_scales.rearrange("o f t -> (o f) t").bitcast(I32))
         word_pool = sb.tile([P, T], I32, name="word_pool", align_bytes=64)
         nc.sync.dma_start(word_pool[:], k_words[0].rearrange("p t b -> p (t b)").bitcast(I32))
         q_raw = []
@@ -39,7 +39,8 @@ def tile_attend_maxsim_kernel(tc, qT, k_words, k_scales, offs, out):
             nc.sync.dma_start(raw[:], qT[0, 512 * o : 512 * (o + 1), :].rearrange("(p j) w -> p j w", j=4))
             q_raw.append(raw)
 
-        nc.vector.memset(scale_pool[0:96, :].bitcast(I32), 0)
+        nc.vector.memset(scale_pool[32:64, :].bitcast(I32), 0)
+        nc.vector.memset(scale_pool[64:P, :].bitcast(I32), 0)
         k_planes = sb.tile([P, PASSES * N], U8, name="k_planes", align_bytes=64)
         nc.vector.memset(k_planes[:].bitcast(I32), 0)
 
@@ -47,21 +48,13 @@ def tile_attend_maxsim_kernel(tc, qT, k_words, k_scales, offs, out):
         nc.vector.tensor_copy(scale_got[:], scale_pool[:].indirect(offsets[:]))
         planes = k_planes[:].bitcast(I32)
         staged = scale_got[:].bitcast(I32)
-
-        def move_rows(quad, o, lo, hi):
-            nc.sync.dma_start(
-                planes[32 * quad : 32 * quad + 4, (o * N + lo) // 4 : (o * N + hi) // 4],
-                staged[96 + 8 * quad + o : 104 + 8 * quad : 2, lo // 4 : hi // 4],
-            )
-
-        for quad in (0, 2):
-            nc.sync.dma_start(planes[32 * quad : 32 * quad + 4, :], staged[96 + 8 * quad : 104 + 8 * quad, :])
-        move_rows(1, 0, 0, N)
-        move_rows(3, 0, 0, N)
-        move_rows(1, 1, 0, N)
-        cuts = [0, 2 * CH, N]
-        for lo, hi in zip(cuts, cuts[1:]):
-            move_rows(3, 1, lo, hi)
+        nc.vector.tensor_copy(planes[0:32, : N // 4], staged[0:32, :])
+        for o, quads in ((0, (2, 1, 3)), (1, (0, 2, 1, 3))):
+            for quad in quads:
+                nc.sync.dma_start(
+                    planes[32 * quad : 32 * quad + 4, o * N // 4 : (o + 1) * N // 4],
+                    staged[16 * o + 4 * quad : 16 * o + 4 * quad + 4, :],
+                )
 
         word_got = sb.tile([P, N], U32, name="word_got", align_bytes=64)
         for h in range(2):

@@ -16,7 +16,7 @@ N, T, D, NQ, SEG = 512, 2048, 1024, 128, 32
 PASSES = 2
 HALF = N // 2
 CH = 128
-SCALAR_SHARE = 96
+HELPER_SHARE = (32, 24)
 FLOPS = 2 * NQ * N * D
 
 
@@ -70,30 +70,47 @@ def tile_attend_maxsim_kernel(tc, qT, k_words, k_scales, offs, out):
         def part_words(codes, o, lo, hi):
             nc.vector.tensor_copy(codes.bitcast(U16), word_halves[:, o, lo:hi])
 
-        def quantise_queries(o):
-            grouped = sb.tile([P, NQ, 4], BF16, name="q_bf%d" % o, align_bytes=64)
-            own = SCALAR_SHARE if o == 1 else NQ
+        q_bf = [sb.tile([P, NQ, 4], BF16, name="q_bf%d" % o, align_bytes=64) for o in range(PASSES)]
+
+        def cast_queries(o):
+            own = NQ - HELPER_SHARE[o]
             nc.scalar.copy(
-                grouped[:, :own, :].rearrange("p (c i) j -> p c j i", i=4),
+                q_bf[o][:, :own, :].rearrange("p (c i) j -> p c j i", i=4),
                 q_raw[o][:, :, :own].rearrange("p j (c i) -> p c j i", i=4),
             )
-            if own < NQ:
+            if o == 0:
+                nc.gpsimd.tensor_scalar(
+                    out=q_bf[o][:, own:, :],
+                    in0=q_raw[o][:, :, own:].rearrange("p j w -> p w j"),
+                    scalar1=1.0,
+                    scalar2=0.0,
+                    op0=mybir.AluOpType.mult,
+                    op1=mybir.AluOpType.add,
+                )
+            elif own < NQ:
                 nc.vector.tensor_copy(
-                    grouped[:, own:, :].rearrange("p (c i) j -> p c j i", i=4),
+                    q_bf[o][:, own:, :].rearrange("p (c i) j -> p c j i", i=4),
                     q_raw[o][:, :, own:].rearrange("p j (c i) -> p c j i", i=4),
                 )
+
+        def quantise_queries(o):
             nc.vector.quantize_mx(
                 out=q_codes[:, o * NQ : (o + 1) * NQ].bitcast(FP8X4),
                 scales=q_planes[:, o * NQ : (o + 1) * NQ],
-                in_=grouped[:].rearrange("p w j -> p (w j)"),
+                in_=q_bf[o][:].rearrange("p w j -> p (w j)"),
             )
 
         k_first = sb.tile([P, 2 * HALF], U8, name="k_first", align_bytes=64)
         part_words(k_first[:], 0, 0, HALF)
+        cast_queries(0)
         quantise_queries(0)
+        cast_queries(1)
         k_rest = sb.tile([P, 2 * N], U8, name="k_rest", tag="stage0", align_bytes=64)
-        part_words(k_rest[:, : 2 * HALF], 0, HALF, N)
-        part_words(k_rest[:, 2 * HALF :], 1, 0, HALF)
+        flat = word_got[:].bitcast(U16)
+        nc.vector.tensor_copy(
+            k_rest[:].bitcast(U16).rearrange("p (a n) -> p a n", a=2),
+            flat[:, 1 : 2 * N - 1].rearrange("p (a m) -> p a m", a=2)[:, :, ::2],
+        )
         quantise_queries(1)
         k_last = sb.tile([P, 2 * HALF], U8, name="k_last", tag="stage1", align_bytes=64)
         part_words(k_last[:], 1, HALF, N)
@@ -103,7 +120,8 @@ def tile_attend_maxsim_kernel(tc, qT, k_words, k_scales, offs, out):
                 return k_first[:, 2 * c0 : 2 * (c0 + CH)]
             if c0 >= N + HALF:
                 return k_last[:, 2 * (c0 - N - HALF) : 2 * (c0 - N - HALF + CH)]
-            return k_rest[:, 2 * (c0 - HALF) : 2 * (c0 - HALF + CH)]
+            at = c0 - N if c0 >= N else c0
+            return k_rest[:, 2 * at : 2 * (at + CH)]
 
         banks = [ps.tile([P, CH], F32, name="bank%d" % g) for g in range(N // CH)]
         best = sb.tile([P, N // SEG], F32, name="best", align_bytes=64)

@@ -16,7 +16,7 @@ N, T, D, NQ, SEG = 512, 2048, 1024, 128, 32
 PASSES = 2
 HALF = N // 2
 CH = 128
-HELPER_SHARE = (32, 24)
+HELPER_SHARE = (32, 48)
 FLOPS = 2 * NQ * N * D
 
 
@@ -27,10 +27,10 @@ def tile_attend_maxsim_kernel(tc, qT, k_words, k_scales, offs, out):
         ps = ctx.enter_context(tc.psum_pool(name="ps", bufs=1))
 
         offsets = sb.tile([P, N // 16], U16, name="offsets")
-        nc.sync.dma_start(offsets[:], offs)
 
         scale_pool = sb.tile([P, T], U8, name="scale_pool", align_bytes=64)
-        nc.sync.dma_start(scale_pool[0:32, :].bitcast(I32), k_scales.rearrange("o f t -> (o f) t").bitcast(I32))
+        nc.sync.dma_start(scale_pool[0:32, :].bitcast(I32), k_scales.rearrange("o f t -> f o t").bitcast(I32))
+        nc.sync.dma_start(offsets[:], offs)
         word_pool = sb.tile([P, T], I32, name="word_pool", align_bytes=64)
         nc.sync.dma_start(word_pool[:], k_words[0].rearrange("p t b -> p (t b)").bitcast(I32))
         q_raw = []
@@ -48,13 +48,17 @@ def tile_attend_maxsim_kernel(tc, qT, k_words, k_scales, offs, out):
         nc.vector.tensor_copy(scale_got[:], scale_pool[:].indirect(offsets[:]))
         planes = k_planes[:].bitcast(I32)
         staged = scale_got[:].bitcast(I32)
-        nc.vector.tensor_copy(planes[0:32, : N // 4], staged[0:32, :])
-        for o, quads in ((0, (2, 1, 3)), (1, (0, 2, 1, 3))):
-            for quad in quads:
-                nc.sync.dma_start(
-                    planes[32 * quad : 32 * quad + 4, o * N // 4 : (o + 1) * N // 4],
-                    staged[16 * o + 4 * quad : 16 * o + 4 * quad + 4, :],
-                )
+        row = N // 4
+        for quad in (0, 2):
+            nc.sync.dma_start(
+                planes[32 * quad : 32 * quad + 4, :].rearrange("r (o n) -> r o n", o=PASSES),
+                staged[8 * quad : 8 * quad + 8, :],
+            )
+        for o, quad, lo, hi in ((0, 1, 0, row), (0, 3, 0, row), (1, 1, 0, row), (1, 3, 0, row // 2), (1, 3, row // 2, row)):
+            nc.sync.dma_start(
+                planes[32 * quad : 32 * quad + 4, o * row + lo : o * row + hi],
+                staged[8 * quad + o : 8 * quad + 8 : 2, lo:hi],
+            )
 
         word_got = sb.tile([P, N], U32, name="word_got", align_bytes=64)
         for h in range(2):
@@ -106,11 +110,8 @@ def tile_attend_maxsim_kernel(tc, qT, k_words, k_scales, offs, out):
         quantise_queries(0)
         cast_queries(1)
         k_rest = sb.tile([P, 2 * N], U8, name="k_rest", tag="stage0", align_bytes=64)
-        flat = word_got[:].bitcast(U16)
-        nc.vector.tensor_copy(
-            k_rest[:].bitcast(U16).rearrange("p (a n) -> p a n", a=2),
-            flat[:, 1 : 2 * N - 1].rearrange("p (a m) -> p a m", a=2)[:, :, ::2],
-        )
+        part_words(k_rest[:, : 2 * HALF], 0, HALF, N)
+        part_words(k_rest[:, 2 * HALF :], 1, 0, HALF)
         quantise_queries(1)
         k_last = sb.tile([P, 2 * HALF], U8, name="k_last", tag="stage1", align_bytes=64)
         part_words(k_last[:], 1, HALF, N)
@@ -120,8 +121,7 @@ def tile_attend_maxsim_kernel(tc, qT, k_words, k_scales, offs, out):
                 return k_first[:, 2 * c0 : 2 * (c0 + CH)]
             if c0 >= N + HALF:
                 return k_last[:, 2 * (c0 - N - HALF) : 2 * (c0 - N - HALF + CH)]
-            at = c0 - N if c0 >= N else c0
-            return k_rest[:, 2 * at : 2 * (at + CH)]
+            return k_rest[:, 2 * (c0 - HALF) : 2 * (c0 - HALF + CH)]
 
         banks = [ps.tile([P, CH], F32, name="bank%d" % g) for g in range(N // CH)]
         best = sb.tile([P, N // SEG], F32, name="best", align_bytes=64)

@@ -14,10 +14,10 @@ FP4X4 = mybir.dt.float4_e2m1fn_x4
 P = 128
 N, T, D, NQ, SEG = 512, 2048, 1024, 128, 32
 PASSES = 2
-HALF = N // 2
 CH = 128
-HELPER_SHARE = (32, 48)
+CHUNKS = N // CH
 FLOPS = 2 * NQ * N * D
+SHARE = (48, 48)
 
 
 def tile_attend_maxsim_kernel(tc, qT, k_words, k_scales, offs, out):
@@ -27,7 +27,6 @@ def tile_attend_maxsim_kernel(tc, qT, k_words, k_scales, offs, out):
         ps = ctx.enter_context(tc.psum_pool(name="ps", bufs=1))
 
         offsets = sb.tile([P, N // 16], U16, name="offsets")
-
         scale_pool = sb.tile([P, T], U8, name="scale_pool", align_bytes=64)
         nc.sync.dma_start(scale_pool[0:32, :].bitcast(I32), k_scales.rearrange("o f t -> f o t").bitcast(I32))
         nc.sync.dma_start(offsets[:], offs)
@@ -60,42 +59,15 @@ def tile_attend_maxsim_kernel(tc, qT, k_words, k_scales, offs, out):
                 staged[8 * quad + o : 8 * quad + 8 : 2, lo:hi],
             )
 
-        word_got = sb.tile([P, N], U32, name="word_got", align_bytes=64)
-        for h in range(2):
-            nc.vector.tensor_copy(
-                word_got[:, h * HALF : (h + 1) * HALF],
-                word_pool[:].bitcast(U32).indirect(offsets[:, h * HALF // 16 : (h + 1) * HALF // 16]),
-            )
+        q_bf = [sb.tile([P, NQ, 4], BF16, name="q_bf%d" % o, align_bytes=64) for o in range(PASSES)]
         q_codes = sb.tile([P, PASSES * NQ], U32, name="q_codes", align_bytes=64)
         q_planes = sb.tile([P, PASSES * NQ], U8, name="q_planes", align_bytes=64)
 
-        word_halves = word_got[:].bitcast(U16).rearrange("p (n o) -> p o n", o=PASSES)
-
-        def part_words(codes, o, lo, hi):
-            nc.vector.tensor_copy(codes.bitcast(U16), word_halves[:, o, lo:hi])
-
-        q_bf = [sb.tile([P, NQ, 4], BF16, name="q_bf%d" % o, align_bytes=64) for o in range(PASSES)]
-
-        def cast_queries(o):
-            own = NQ - HELPER_SHARE[o]
-            nc.scalar.copy(
-                q_bf[o][:, :own, :].rearrange("p (c i) j -> p c j i", i=4),
-                q_raw[o][:, :, :own].rearrange("p j (c i) -> p c j i", i=4),
+        def cast_queries(copy, o, lo, hi):
+            copy(
+                q_bf[o][:, lo:hi, :].rearrange("p (c i) j -> p c j i", i=4),
+                q_raw[o][:, :, lo:hi].rearrange("p j (c i) -> p c j i", i=4),
             )
-            if o == 0:
-                nc.gpsimd.tensor_scalar(
-                    out=q_bf[o][:, own:, :],
-                    in0=q_raw[o][:, :, own:].rearrange("p j w -> p w j"),
-                    scalar1=1.0,
-                    scalar2=0.0,
-                    op0=mybir.AluOpType.mult,
-                    op1=mybir.AluOpType.add,
-                )
-            elif own < NQ:
-                nc.vector.tensor_copy(
-                    q_bf[o][:, own:, :].rearrange("p (c i) j -> p c j i", i=4),
-                    q_raw[o][:, :, own:].rearrange("p j (c i) -> p c j i", i=4),
-                )
 
         def quantise_queries(o):
             nc.vector.quantize_mx(
@@ -104,41 +76,59 @@ def tile_attend_maxsim_kernel(tc, qT, k_words, k_scales, offs, out):
                 in_=q_bf[o][:].rearrange("p w j -> p (w j)"),
             )
 
-        k_first = sb.tile([P, 2 * HALF], U8, name="k_first", align_bytes=64)
-        part_words(k_first[:], 0, 0, HALF)
-        cast_queries(0)
+        word_got = {}
+        k_codes = {}
+
+        def gather_words(g, tag):
+            word_got[g] = sb.tile([P, CH], U32, name="word_got%d" % g, tag=tag, align_bytes=64)
+            nc.vector.tensor_copy(
+                word_got[g][:], word_pool[:].bitcast(U32).indirect(offsets[:, g * CH // 16 : (g + 1) * CH // 16])
+            )
+
+        def halves(g):
+            return word_got[g][:].bitcast(U16).rearrange("p (n o) -> p o n", o=PASSES)
+
+        def part_words(codes, o, g):
+            nc.vector.tensor_copy(codes.bitcast(U16), halves(g)[:, o, :])
+            k_codes[(o, g)] = codes
+
+        for o in range(PASSES):
+            cast_queries(nc.scalar.copy, o, 0, NQ - SHARE[o])
+        for g in range(CHUNKS - 1):
+            gather_words(g, "word_got%d" % g)
+        k_first = sb.tile([P, PASSES, 2 * CH], U8, name="k_first", align_bytes=64)
+        nc.vector.tensor_copy(k_first[:].bitcast(U16), halves(0))
+        for o in range(PASSES):
+            k_codes[(o, 0)] = k_first[:, o, :]
+        cast_queries(nc.vector.tensor_copy, 0, NQ - SHARE[0], NQ)
+        gather_words(CHUNKS - 1, "word_got0")
         quantise_queries(0)
-        cast_queries(1)
-        k_rest = sb.tile([P, 2 * N], U8, name="k_rest", tag="stage0", align_bytes=64)
-        part_words(k_rest[:, : 2 * HALF], 0, HALF, N)
-        part_words(k_rest[:, 2 * HALF :], 1, 0, HALF)
+        k_rest = sb.tile([P, 4, 2 * CH], U8, name="k_rest", tag="stage0", align_bytes=64)
+        part_words(k_rest[:, 0, :], 0, 1)
+        cast_queries(nc.vector.tensor_copy, 1, NQ - SHARE[1], NQ)
+        part_words(k_rest[:, 1, :], 0, 2)
+        part_words(k_rest[:, 2, :], 0, 3)
+        part_words(k_rest[:, 3, :], 1, 1)
         quantise_queries(1)
-        k_last = sb.tile([P, 2 * HALF], U8, name="k_last", tag="stage1", align_bytes=64)
-        part_words(k_last[:], 1, HALF, N)
+        k_last = sb.tile([P, 2, 2 * CH], U8, name="k_last", tag="stage1", align_bytes=64)
+        part_words(k_last[:, 0, :], 1, 2)
+        part_words(k_last[:, 1, :], 1, 3)
 
-        def k_codes(c0):
-            if c0 < HALF:
-                return k_first[:, 2 * c0 : 2 * (c0 + CH)]
-            if c0 >= N + HALF:
-                return k_last[:, 2 * (c0 - N - HALF) : 2 * (c0 - N - HALF + CH)]
-            return k_rest[:, 2 * (c0 - HALF) : 2 * (c0 - HALF + CH)]
-
-        banks = [ps.tile([P, CH], F32, name="bank%d" % g) for g in range(N // CH)]
+        banks = [ps.tile([P, CH], F32, name="bank%d" % g) for g in range(CHUNKS)]
         best = sb.tile([P, N // SEG], F32, name="best", align_bytes=64)
         for o in range(PASSES):
-            for g in range(N // CH):
-                c0 = o * N + g * CH
+            for g in range(CHUNKS):
                 nc.tensor.matmul_mx(
                     out=banks[g][:],
                     lhsT=q_codes[:, o * NQ : (o + 1) * NQ].bitcast(FP8X4),
                     lhsT_scale=q_planes[:, o * NQ : (o + 1) * NQ],
-                    rhs=k_codes(c0).bitcast(FP4X4),
-                    rhs_scale=k_planes[:, c0 : c0 + CH],
+                    rhs=k_codes[(o, g)].bitcast(FP4X4),
+                    rhs_scale=k_planes[:, o * N + g * CH : o * N + (g + 1) * CH],
                     start=(o == 0),
                     stop=(o == PASSES - 1),
                 )
         per = CH // SEG
-        for g in range(N // CH):
+        for g in range(CHUNKS):
             nc.vector.tensor_reduce(
                 out=best[:, g * per : (g + 1) * per],
                 in_=banks[g][:].rearrange("p (j s) -> p j s", s=SEG),

@@ -17,7 +17,7 @@ PASSES = 2
 CH = 128
 CHUNKS = N // CH
 FLOPS = 2 * NQ * N * D
-SHARE = (48, 48)
+SHARE = (32, 48)
 
 
 def tile_attend_maxsim_kernel(tc, qT, k_words, k_scales, offs, out):
@@ -96,19 +96,19 @@ def tile_attend_maxsim_kernel(tc, qT, k_words, k_scales, offs, out):
             cast_queries(nc.scalar.copy, o, 0, NQ - SHARE[o])
         for g in range(CHUNKS - 1):
             gather_words(g, "word_got%d" % g)
-        k_first = sb.tile([P, PASSES, 2 * CH], U8, name="k_first", align_bytes=64)
-        nc.vector.tensor_copy(k_first[:].bitcast(U16), halves(0))
+        k_first = sb.tile([P, 3, 2 * CH], U8, name="k_first", align_bytes=64)
+        nc.vector.tensor_copy(k_first[:, :PASSES, :].bitcast(U16), halves(0))
         for o in range(PASSES):
             k_codes[(o, 0)] = k_first[:, o, :]
         cast_queries(nc.vector.tensor_copy, 0, NQ - SHARE[0], NQ)
+        part_words(k_first[:, 2, :], 0, 1)
         gather_words(CHUNKS - 1, "word_got0")
         quantise_queries(0)
-        k_rest = sb.tile([P, 4, 2 * CH], U8, name="k_rest", tag="stage0", align_bytes=64)
-        part_words(k_rest[:, 0, :], 0, 1)
         cast_queries(nc.vector.tensor_copy, 1, NQ - SHARE[1], NQ)
-        part_words(k_rest[:, 1, :], 0, 2)
-        part_words(k_rest[:, 2, :], 0, 3)
-        part_words(k_rest[:, 3, :], 1, 1)
+        k_rest = sb.tile([P, 3, 2 * CH], U8, name="k_rest", tag="stage0", align_bytes=64)
+        part_words(k_rest[:, 0, :], 0, 2)
+        part_words(k_rest[:, 1, :], 0, 3)
+        part_words(k_rest[:, 2, :], 1, 1)
         quantise_queries(1)
         k_last = sb.tile([P, 2, 2 * CH], U8, name="k_last", tag="stage1", align_bytes=64)
         part_words(k_last[:, 0, :], 1, 2)

@@ -28,7 +28,7 @@ def tile_attend_maxsim_kernel(tc, qT, k_words, k_scales, offs, out):
 
         offsets = sb.tile([P, N // 16], U16, name="offsets")
         scale_pool = sb.tile([P, T], U8, name="scale_pool", align_bytes=64)
-        nc.sync.dma_start(scale_pool[0:32, :].bitcast(I32), k_scales.rearrange("o f t -> f o t").bitcast(I32))
+        nc.sync.dma_start(scale_pool[0:32, :].bitcast(I32), k_scales.rearrange("o f t -> (o f) t").bitcast(I32))
         nc.sync.dma_start(offsets[:], offs)
         word_pool = sb.tile([P, T], I32, name="word_pool", align_bytes=64)
         nc.sync.dma_start(word_pool[:], k_words[0].rearrange("p t b -> p (t b)").bitcast(I32))
@@ -48,16 +48,13 @@ def tile_attend_maxsim_kernel(tc, qT, k_words, k_scales, offs, out):
         planes = k_planes[:].bitcast(I32)
         staged = scale_got[:].bitcast(I32)
         row = N // 4
-        for quad in (0, 2):
-            nc.sync.dma_start(
-                planes[32 * quad : 32 * quad + 4, :].rearrange("r (o n) -> r o n", o=PASSES),
-                staged[8 * quad : 8 * quad + 8, :],
-            )
-        for o, quad, lo, hi in ((0, 1, 0, row), (0, 3, 0, row), (1, 1, 0, row), (1, 3, 0, row // 2), (1, 3, row // 2, row)):
-            nc.sync.dma_start(
-                planes[32 * quad : 32 * quad + 4, o * row + lo : o * row + hi],
-                staged[8 * quad + o : 8 * quad + 8 : 2, lo:hi],
-            )
+        nc.vector.tensor_copy(planes[0:4, :row], staged[0:4, :])
+        for o in range(PASSES):
+            for quad in (0, 2, 1, 3)[1 - o :]:
+                nc.sync.dma_start(
+                    planes[32 * quad : 32 * quad + 4, o * row : (o + 1) * row],
+                    staged[16 * o + 4 * quad : 16 * o + 4 * quad + 4, :],
+                )
 
         q_bf = [sb.tile([P, NQ, 4], BF16, name="q_bf%d" % o, align_bytes=64) for o in range(PASSES)]
         q_codes = sb.tile([P, PASSES * NQ], U32, name="q_codes", align_bytes=64)

from contextlib import ExitStack

import concourse.mybir as mybir

F32 = mybir.dt.float32
BF16 = mybir.dt.bfloat16
I32 = mybir.dt.int32
U32 = mybir.dt.uint32
U16 = mybir.dt.uint16
U8 = mybir.dt.uint8
FP8X4 = mybir.dt.float8_e4m3fn_x4
FP4X4 = mybir.dt.float4_e2m1fn_x4

P = 128
N, T, D, NQ, SEG = 512, 2048, 1024, 128, 32
PASSES = 2
CH = 128
CHUNKS = N // CH
FLOPS = 2 * NQ * N * D
SHARE = (32, 48)


def tile_attend_maxsim_kernel(tc, qT, k_words, k_scales, offs, out):
    nc = tc.nc
    with ExitStack() as ctx:
        sb = ctx.enter_context(tc.tile_pool(name="sb", bufs=1))
        ps = ctx.enter_context(tc.psum_pool(name="ps", bufs=1))

        offsets = sb.tile([P, N // 16], U16, name="offsets")
        scale_pool = sb.tile([P, T], U8, name="scale_pool", align_bytes=64)
        nc.sync.dma_start(scale_pool[0:32, :].bitcast(I32), k_scales.rearrange("o f t -> (o f) t").bitcast(I32))
        nc.sync.dma_start(offsets[:], offs)
        word_pool = sb.tile([P, T], I32, name="word_pool", align_bytes=64)
        nc.sync.dma_start(word_pool[:], k_words[0].rearrange("p t b -> p (t b)").bitcast(I32))
        q_raw = []
        for o in range(PASSES):
            raw = sb.tile([P, 4, NQ], F32, name="q_raw%d" % o, tag="stage%d" % o, align_bytes=64)
            nc.sync.dma_start(raw[:], qT[0, 512 * o : 512 * (o + 1), :].rearrange("(p j) w -> p j w", j=4))
            q_raw.append(raw)

        nc.vector.memset(scale_pool[32:64, :].bitcast(I32), 0)
        nc.vector.memset(scale_pool[64:P, :].bitcast(I32), 0)
        k_planes = sb.tile([P, PASSES * N], U8, name="k_planes", align_bytes=64)
        nc.vector.memset(k_planes[:].bitcast(I32), 0)

        scale_got = sb.tile([P, N], U8, name="scale_got", align_bytes=64)
        nc.vector.tensor_copy(scale_got[:], scale_pool[:].indirect(offsets[:]))
        planes = k_planes[:].bitcast(I32)
        staged = scale_got[:].bitcast(I32)
        row = N // 4
        nc.vector.tensor_copy(planes[0:4, :row], staged[0:4, :])
        for o in range(PASSES):
            for quad in (0, 2, 1, 3)[1 - o :]:
                nc.sync.dma_start(
                    planes[32 * quad : 32 * quad + 4, o * row : (o + 1) * row],
                    staged[16 * o + 4 * quad : 16 * o + 4 * quad + 4, :],
                )

        q_bf = [sb.tile([P, NQ, 4], BF16, name="q_bf%d" % o, align_bytes=64) for o in range(PASSES)]
        q_codes = sb.tile([P, PASSES * NQ], U32, name="q_codes", align_bytes=64)
        q_planes = sb.tile([P, PASSES * NQ], U8, name="q_planes", align_bytes=64)

        def cast_queries(copy, o, lo, hi):
            copy(
                q_bf[o][:, lo:hi, :].rearrange("p (c i) j -> p c j i", i=4),
                q_raw[o][:, :, lo:hi].rearrange("p j (c i) -> p c j i", i=4),
            )

        def quantise_queries(o):
            nc.vector.quantize_mx(
                out=q_codes[:, o * NQ : (o + 1) * NQ].bitcast(FP8X4),
                scales=q_planes[:, o * NQ : (o + 1) * NQ],
                in_=q_bf[o][:].rearrange("p w j -> p (w j)"),
            )

        word_got = {}
        k_codes = {}

        def gather_words(g, tag):
            word_got[g] = sb.tile([P, CH], U32, name="word_got%d" % g, tag=tag, align_bytes=64)
            nc.vector.tensor_copy(
                word_got[g][:], word_pool[:].bitcast(U32).indirect(offsets[:, g * CH // 16 : (g + 1) * CH // 16])
            )

        def halves(g):
            return word_got[g][:].bitcast(U16).rearrange("p (n o) -> p o n", o=PASSES)

        def part_words(codes, o, g):
            nc.vector.tensor_copy(codes.bitcast(U16), halves(g)[:, o, :])
            k_codes[(o, g)] = codes

        for o in range(PASSES):
            cast_queries(nc.scalar.copy, o, 0, NQ - SHARE[o])
        for g in range(CHUNKS - 1):
            gather_words(g, "word_got%d" % g)
        k_first = sb.tile([P, 3, 2 * CH], U8, name="k_first", align_bytes=64)
        nc.vector.tensor_copy(k_first[:, :PASSES, :].bitcast(U16), halves(0))
        for o in range(PASSES):
            k_codes[(o, 0)] = k_first[:, o, :]
        cast_queries(nc.vector.tensor_copy, 0, NQ - SHARE[0], NQ)
        part_words(k_first[:, 2, :], 0, 1)
        gather_words(CHUNKS - 1, "word_got0")
        quantise_queries(0)
        cast_queries(nc.vector.tensor_copy, 1, NQ - SHARE[1], NQ)
        k_rest = sb.tile([P, 3, 2 * CH], U8, name="k_rest", tag="stage0", align_bytes=64)
        part_words(k_rest[:, 0, :], 0, 2)
        part_words(k_rest[:, 1, :], 0, 3)
        part_words(k_rest[:, 2, :], 1, 1)
        quantise_queries(1)
        k_last = sb.tile([P, 2, 2 * CH], U8, name="k_last", tag="stage1", align_bytes=64)
        part_words(k_last[:, 0, :], 1, 2)
        part_words(k_last[:, 1, :], 1, 3)

        banks = [ps.tile([P, CH], F32, name="bank%d" % g) for g in range(CHUNKS)]
        best = sb.tile([P, N // SEG], F32, name="best", align_bytes=64)
        for o in range(PASSES):
            for g in range(CHUNKS):
                nc.tensor.matmul_mx(
                    out=banks[g][:],
                    lhsT=q_codes[:, o * NQ : (o + 1) * NQ].bitcast(FP8X4),
                    lhsT_scale=q_planes[:, o * NQ : (o + 1) * NQ],
                    rhs=k_codes[(o, g)].bitcast(FP4X4),
                    rhs_scale=k_planes[:, o * N + g * CH : o * N + (g + 1) * CH],
                    start=(o == 0),
                    stop=(o == PASSES - 1),
                )
        per = CH // SEG
        for g in range(CHUNKS):
            nc.vector.tensor_reduce(
                out=best[:, g * per : (g + 1) * per],
                in_=banks[g][:].rearrange("p (j s) -> p j s", s=SEG),
                axis=mybir.AxisListType.X,
                op=mybir.AluOpType.max,
            )
        nc.sync.dma_start(out[0], best[:])
